import numpy as np
import ml_dtypes


def mxq(x, axis, fmt="e4m3"):
    dtype, down = {"e4m3": (ml_dtypes.float8_e4m3fn, 7), "e5m2": (ml_dtypes.float8_e5m2, 14)}[fmt]
    v = np.moveaxis(np.asarray(x, np.float32).astype(ml_dtypes.bfloat16).astype(np.float64), axis, -1)
    blocks = v.reshape(v.shape[:-1] + (-1, 32))
    amax = np.abs(blocks).max(-1, keepdims=True)
    byte = np.maximum(np.where(amax > 0, np.frexp(amax)[1] - 1 + 127, 0) - down, 1)
    scale = np.exp2(byte - 127.0)
    codes = (blocks / scale).astype(np.float32).astype(dtype).astype(np.float64)
    return np.moveaxis((codes * scale).reshape(v.shape), -1, axis)


WIDE = False


def mx_kscale(k):
    if not WIDE:
        return np.ones(k)
    levels = np.array([30, -30])
    if k % 512:
        return np.exp2(np.random.permutation(np.resize(levels, k // 32))).repeat(32)
    a = np.empty((k // 512, 16))
    for p in range(k // 512):
        a[p, :8] = np.random.permutation(np.resize(levels, 8))
        for g in range(8):
            far = levels[np.abs(levels - a[p, g]) >= 10]
            a[p, g + 8] = far[np.random.randint(len(far))]
    return np.exp2(a.ravel()).repeat(32)


BF16 = ml_dtypes.bfloat16


def bf(x):
    return np.asarray(x, np.float32).astype(BF16)


def f64(x):
    return np.asarray(x).astype(np.float64)


E2M1 = np.array([0.0, 0.5, 1.0, 1.5, 2.0, 3.0, 4.0, 6.0, -0.0, -0.5, -1.0, -1.5, -2.0, -3.0, -4.0, -6.0])


def pack_weight(w, fmt):
    k, n = w.shape
    w = f64(bf(w)).reshape(k // 32, 32, n)
    amax = np.abs(w).max(1)
    if fmt in ("e4m3", "e5m2"):
        byte = np.frexp(amax)[1] - 1 + 127 - (7 if fmt == "e4m3" else 14)
    else:
        mant, ex = np.frexp(amax / 6.0)
        byte = np.where(mant > 0.5, ex, ex - 1) + 127
    byte = np.clip(np.where(amax > 0, byte, 1), 1, 254)
    scaled = (w * np.exp2(127.0 - byte)[:, None, :]).reshape(k, n).astype(np.float32)
    by_word = np.ascontiguousarray(scaled.reshape(k // 512, 128, 4, n).transpose(0, 1, 3, 2))
    if fmt in ("e4m3", "e5m2"):
        words = by_word.astype(ml_dtypes.float8_e4m3fn if fmt == "e4m3" else ml_dtypes.float8_e5m2).view(np.uint8)
    else:
        c = by_word.astype(ml_dtypes.float4_e2m1fn).view(np.uint8) & 0xF
        words = c[..., 0::2] | (c[..., 1::2] << 4)
    return np.ascontiguousarray(words), np.ascontiguousarray(byte.astype(np.uint8).reshape(k // 512, 16, n))


def unpack_weight(words, scales, fmt):
    g, p, n, _ = words.shape
    if fmt in ("e4m3", "e5m2"):
        vals = np.ascontiguousarray(words).view(ml_dtypes.float8_e4m3fn if fmt == "e4m3" else ml_dtypes.float8_e5m2).astype(np.float64)
    else:
        nib = np.empty((g, p, n, 4), np.uint8)
        nib[..., 0::2] = words & 0xF
        nib[..., 1::2] = words >> 4
        vals = E2M1[nib]
    vals = vals * np.repeat(np.exp2(scales.astype(np.float64) - 127.0), 8, axis=1)[..., None]
    return vals.transpose(0, 1, 3, 2).reshape(g * 512, n)


M, D, T, C = 1024, 512, 2048, 2

APERTURE = 8.0
COSINE = 0.7


def setup_inputs():
    s = mx_kscale(M)
    px, py = np.random.uniform(-APERTURE, APERTURE, M), np.random.uniform(-APERTURE, APERTURE, M)
    ux, uy = np.random.uniform(-COSINE, COSINE, D), np.random.uniform(-COSINE, COSINE, D)
    phase = 2.0 * np.pi * (px[:, None] * ux[None, :] + py[:, None] * uy[None, :])
    norm = s[:, None] / np.sqrt(M)
    r_re_words, r_re_scales = pack_weight(np.random.standard_t(5, (M, T)) / s[:, None], "e5m2")
    r_im_words, r_im_scales = pack_weight(np.random.standard_t(5, (M, T)) / s[:, None], "e5m2")
    return {"a_re": bf(np.cos(phase) * norm),
            "a_im": bf(np.sin(phase) * norm),
            "r_re_words": r_re_words, "r_re_scales": r_re_scales,
            "r_im_words": r_im_words, "r_im_scales": r_im_scales,
            "step": bf(1.0 + 0.1 * np.random.standard_normal(D)),
            "amp": bf(np.random.standard_normal((C, D, T)))}


def reference(a_re, a_im, r_re_words, r_re_scales, r_im_words, r_im_scales, step, amp):
    ar = mxq(f64(a_re), 0, "e4m3")
    ai = mxq(f64(a_im), 0, "e4m3")
    rr = unpack_weight(r_re_words, r_re_scales, "e5m2")
    ri = unpack_weight(r_im_words, r_im_scales, "e5m2")
    re = (ar.T @ rr) + (ai.T @ ri)
    im = (ar.T @ ri) - (ai.T @ rr)
    return f64(amp) + f64(step)[None, :, None] * np.stack([re, im])

@@ -1,0 +1,256 @@
+from contextlib import ExitStack
+
+import concourse.mybir as mybir
+from concourse.masks import make_identity
+
+M, D, T, C = 1024, 512, 2048, 2
+FLOPS = 4 * 2 * M * D * T
+
+F32 = mybir.dt.float32
+BF16 = mybir.dt.bfloat16
+I32 = mybir.dt.int32
+U32 = mybir.dt.uint32
+U8 = mybir.dt.uint8
+E4X4 = mybir.dt.float8_e4m3fn_x4
+E5X4 = mybir.dt.float8_e5m2_x4
+ALU = mybir.AluOpType
+
+P = 128
+PACK = 4
+K_PASS = P * PACK
+G = M // K_PASS
+MT = D // P
+NT = 512
+HALF_T = T // 2
+RE, IM = 0, 1
+
+
+def tile_steering_residual_step_e2_kernel(
+    tc, a_re, a_im, r_re_words, r_re_scales, r_im_words, r_im_scales, step, amp, out
+):
+    nc = tc.nc
+    a_in = (a_re, a_im)
+    words_in = (r_re_words, r_im_words)
+    scales_in = (r_re_scales, r_im_scales)
+
+    with ExitStack() as ctx:
+        keep = ctx.enter_context(tc.tile_pool(name="keep", bufs=1))
+        psum = ctx.enter_context(tc.psum_pool(name="psum", bufs=1))
+        ctx.enter_context(tc.manual_schedule())
+
+        def sb(label, shape, dtype):
+            return keep.tile(shape, dtype, name=label, align_bytes=64)
+
+        raw = {}
+        grp = {}
+        codes = {}
+        cscale = {}
+        for part in (RE, IM):
+            for g in range(G):
+                raw[part, g] = sb(f"raw{part}{g}", [P, PACK, D], BF16)
+                for sign in ((1,) if part == RE else (1, -1)):
+                    for hf in (0, 1):
+                        key = (part, g, sign, hf)
+                        lab = f"{part}{g}{sign + 1}{hf}"
+                        grp[key] = sb("grp" + lab, [P, D // 2, PACK], BF16)
+                        codes[key] = sb("codes" + lab, [P, D // 2], U32)
+                        cscale[key] = sb("cscale" + lab, [P, D // 2], U8)
+        chunks = ((0, 512), (512, 512), (1024, 1024))
+        words = {}
+        for part in (RE, IM):
+            for g in range(G):
+                for i, (c0, w) in enumerate(chunks):
+                    words[part, g, i] = sb(f"words{part}{g}{i}", [P, w], I32)
+        schunks = ((0, 512), (512, 1536))
+        rscale = {}
+        for part in (RE, IM):
+            for i, (c0, w) in enumerate(schunks):
+                rscale[part, i] = sb(f"rscale{part}{i}", [P, G, w], U8)
+        amps = {}
+        outs = {}
+        for h in (0, 1):
+            for m in range(MT):
+                amps[h, m] = sb(f"amp{h}{m}", [P, C, HALF_T], BF16)
+                for c in (RE, IM):
+                    outs[h, m, c] = sb(f"out{h}{m}{c}", [P, HALF_T], F32)
+        step_rows = sb("step_rows", [P, P], BF16)
+        ident = sb("ident", [P, P], BF16)
+        step_col = sb("step_col", [P, MT], F32)
+
+        def load_a(part, g):
+            nc.sync.dma_start(
+                out=raw[part, g][:],
+                in_=a_in[part][g * K_PASS : (g + 1) * K_PASS, :].rearrange("(p j) d -> p j d", j=PACK),
+            )
+
+        def load_words(part, g, i):
+            c0, w = chunks[i]
+            flat = words_in[part][g].rearrange("p n t -> p (n t)")
+            nc.sync.dma_start(
+                out=words[part, g, i][:], in_=flat[:, PACK * c0 : PACK * (c0 + w)].bitcast(I32)
+            )
+
+        def load_scales(eng, part, i):
+            c0, w = schunks[i]
+            for q in range(4):
+                eng.dma_start(
+                    out=rscale[part, i][32 * q : 32 * q + 4, :, :].bitcast(I32),
+                    in_=scales_in[part][:, 4 * q : 4 * q + 4, c0 : c0 + w].rearrange("g q n -> q g n").bitcast(I32),
+                )
+
+        def load_amp(h, m):
+            nc.sync.dma_start(
+                out=amps[h, m][:],
+                in_=amp[:, m * P : (m + 1) * P, h * HALF_T : (h + 1) * HALF_T].rearrange("c p n -> p c n"),
+            )
+
+        load_a(RE, 0)
+        for i in (0, 1):
+            for part in (RE, IM):
+                nc.vector.memset(rscale[part, i][:].rearrange("p g n -> p (g n)").bitcast(I32), 0)
+        nc.vector.memset(step_rows[:], 0.0)
+        nc.scalar.dma_start(out=step_rows[0:MT, :], in_=step.rearrange("(m p) -> m p", p=P))
+        load_words(RE, 0, 0)
+        load_scales(nc.sync, RE, 0)
+        make_identity(nc, ident[:])
+        load_scales(nc.gpsimd, IM, 0)
+        load_words(IM, 0, 0)
+        load_a(IM, 0)
+        load_a(RE, 1)
+        load_words(RE, 1, 0)
+        load_words(IM, 1, 0)
+        load_a(IM, 1)
+        load_scales(nc.sync, RE, 1)
+        load_scales(nc.sync, IM, 1)
+        for g in range(G):
+            for part in (RE, IM):
+                load_words(part, g, 1)
+        for m in range(MT):
+            load_amp(0, m)
+        for g in range(G):
+            for part in (RE, IM):
+                load_words(part, g, 2)
+        for m in range(MT):
+            load_amp(1, m)
+
+        step_t = psum.tile([P, P], BF16, name="bank7")
+        nc.tensor.transpose(step_t[:], step_rows[:], ident[:])
+        nc.scalar.copy(step_col[:], step_t[:, 0:MT])
+
+        H2 = D // 2
+
+        def interleave(eng_copy, part, g, hf, lo=0, hi=H2):
+            eng_copy(
+                out=grp[part, g, 1, hf][:, lo:hi, :],
+                in_=raw[part, g][:, :, hf * H2 + lo : hf * H2 + hi].rearrange("p j d -> p d j"),
+            )
+
+        def scopy(out, in_):
+            nc.scalar.copy(out, in_)
+
+        def vcopy(out, in_):
+            nc.vector.tensor_copy(out=out, in_=in_)
+
+        def negate(part, g, hf):
+            nc.vector.tensor_scalar(
+                out=grp[part, g, -1, hf][:], in0=grp[part, g, 1, hf][:], scalar1=-1.0, scalar2=None, op0=ALU.mult
+            )
+
+        def quantize(part, g, sign, hf, lo=0, hi=H2):
+            key = (part, g, sign, hf)
+            nc.vector.quantize_mx(
+                out=codes[key][:, lo:hi].bitcast(E4X4),
+                scales=cscale[key][:, lo:hi],
+                in_=grp[key][:, lo:hi, :].rearrange("p d j -> p (d j)"),
+            )
+
+        def mm(bank, m, n0, apart, sign, rpart, g, start, stop):
+            key = (apart, g, sign, m // 2)
+            ac = slice((m % 2) * P, (m % 2 + 1) * P)
+            i = 0 if n0 < 512 else (1 if n0 < 1024 else 2)
+            wc = n0 - chunks[i][0]
+            si = 0 if n0 < 512 else 1
+            sc = n0 - schunks[si][0]
+            nc.tensor.matmul_mx(
+                out=bank[:],
+                lhsT=codes[key][:, ac].bitcast(E4X4),
+                lhsT_scale=cscale[key][:, ac],
+                rhs=words[rpart, g, i][:, wc : wc + NT].bitcast(E5X4),
+                rhs_scale=rscale[rpart, si][:, g, sc : sc + NT],
+                start=start,
+                stop=stop,
+            )
+
+        def new_bank(k):
+            return psum.tile([P, NT], F32, name=f"bank{k}")
+
+        def finish(bank, h, m, c, n0):
+            cols = slice(n0 - h * HALF_T, n0 - h * HALF_T + NT)
+            nc.vector.scalar_tensor_tensor(
+                out=outs[h, m, c][:, cols],
+                in0=bank[:],
+                scalar=step_col[:, m : m + 1],
+                in1=amps[h, m][:, c, cols],
+                op0=ALU.mult,
+                op1=ALU.add,
+            )
+
+        def store(h, m, c, c0, w):
+            nc.sync.dma_start(
+                out=out[c, m * P : (m + 1) * P, h * HALF_T + c0 : h * HALF_T + c0 + w],
+                in_=outs[h, m, c][:, c0 : c0 + w],
+            )
+
+        banks = {}
+        for g in range(G):
+            interleave(scopy, RE, g, 1)
+            if g == 0:
+                interleave(vcopy, RE, g, 0, 0, P)
+                interleave(vcopy, RE, g, 0, P, H2)
+                quantize(RE, g, 1, 0, 0, P)
+                quantize(RE, g, 1, 0, P, H2)
+            else:
+                interleave(vcopy, RE, g, 0)
+                quantize(RE, g, 1, 0)
+            quantize(RE, g, 1, 1)
+            for c in (RE, IM):
+                for m in range(MT):
+                    if g == 0:
+                        banks[m, c] = new_bank(2 * m + c)
+                    mm(banks[m, c], m, 0, RE, 1, RE if c == RE else IM, g, g == 0, False)
+            interleave(scopy, IM, g, 1)
+            interleave(vcopy, IM, g, 0)
+            for hf in (0, 1):
+                negate(IM, g, hf)
+                quantize(IM, g, 1, hf)
+                quantize(IM, g, -1, hf)
+            for m in range(MT):
+                mm(banks[m, RE], m, 0, IM, 1, IM, g, False, g == G - 1)
+                mm(banks[m, IM], m, 0, IM, -1, RE, g, False, g == G - 1)
+        for m in range(MT):
+            for c in (RE, IM):
+                finish(banks[m, c], 0, m, c, 0)
+
+        def product(bank, m, c, n0):
+            order = [(apart, g) for apart in (RE, IM) for g in range(G)]
+            for i, (apart, g) in enumerate(order):
+                sign = -1 if (apart == IM and c == IM) else 1
+                rpart = apart if c == RE else 1 - apart
+                mm(bank, m, n0, apart, sign, rpart, g, i == 0, i == len(order) - 1)
+
+        for m in range(MT):
+            for c in (RE, IM):
+                bank = new_bank(2 * m + c)
+                product(bank, m, c, NT)
+                finish(bank, 0, m, c, NT)
+                store(0, m, c, 0, HALF_T)
+        for m in range(MT):
+            for c in (RE, IM):
+                for nb in (0, 1):
+                    bank = new_bank((4 * m + 2 * c + nb) % 8)
+                    product(bank, m, c, HALF_T + nb * NT)
+                    finish(bank, 1, m, c, HALF_T + nb * NT)
+                    if m == MT - 1:
+                        store(1, m, c, nb * NT, NT)
+                if m < MT - 1:
+                    store(1, m, c, 0, HALF_T)

@@ -104,27 +104,32 @@ def tile_steering_residual_step_e2_kernel(
                 in_=amp[:, m * P : (m + 1) * P, h * HALF_T : (h + 1) * HALF_T].rearrange("c p n -> p c n"),
             )
 
+        def clear_scales(part, i):
+            nc.vector.memset(rscale[part, i][:].rearrange("p g n -> p (g n)").bitcast(I32), 0)
+
         load_a(RE, 0)
-        for i in (0, 1):
-            for part in (RE, IM):
-                nc.vector.memset(rscale[part, i][:].rearrange("p g n -> p (g n)").bitcast(I32), 0)
         nc.vector.memset(step_rows[:], 0.0)
-        nc.scalar.dma_start(out=step_rows[0:MT, :], in_=step.rearrange("(m p) -> m p", p=P))
-        load_words(RE, 0, 0)
-        load_scales(nc.sync, RE, 0)
+        clear_scales(RE, 0)
+        clear_scales(IM, 0)
+        clear_scales(RE, 1)
+        clear_scales(IM, 1)
+        nc.gpsimd.dma_start(out=step_rows[0:MT, :], in_=step.rearrange("(m p) -> m p", p=P))
         make_identity(nc, ident[:])
-        load_scales(nc.gpsimd, IM, 0)
+        load_scales(nc.sync, RE, 0)
+        load_words(RE, 0, 0)
         load_words(IM, 0, 0)
         load_a(IM, 0)
+        load_scales(nc.sync, IM, 0)
         load_a(RE, 1)
+        load_a(IM, 1)
         load_words(RE, 1, 0)
         load_words(IM, 1, 0)
-        load_a(IM, 1)
+        load_words(RE, 0, 1)
         load_scales(nc.sync, RE, 1)
+        load_words(IM, 0, 1)
+        load_words(RE, 1, 1)
         load_scales(nc.sync, IM, 1)
-        for g in range(G):
-            for part in (RE, IM):
-                load_words(part, g, 1)
+        load_words(IM, 1, 1)
         for m in range(MT):
             load_amp(0, m)
         for g in range(G):
@@ -132,10 +137,6 @@ def tile_steering_residual_step_e2_kernel(
                 load_words(part, g, 2)
         for m in range(MT):
             load_amp(1, m)
-
-        step_t = psum.tile([P, P], BF16, name="bank7")
-        nc.tensor.transpose(step_t[:], step_rows[:], ident[:])
-        nc.scalar.copy(step_col[:], step_t[:, 0:MT])
 
         H2 = D // 2
 
@@ -184,49 +185,69 @@ def tile_steering_residual_step_e2_kernel(
         def new_bank(k):
             return psum.tile([P, NT], F32, name=f"bank{k}")
 
-        def finish(bank, h, m, c, n0):
-            cols = slice(n0 - h * HALF_T, n0 - h * HALF_T + NT)
+        def finish(bank, h, m, c, n0, lo=0, w=NT):
+            cols = slice(n0 - h * HALF_T + lo, n0 - h * HALF_T + lo + w)
             nc.vector.scalar_tensor_tensor(
                 out=outs[h, m, c][:, cols],
-                in0=bank[:],
+                in0=bank[:, lo : lo + w],
                 scalar=step_col[:, m : m + 1],
                 in1=amps[h, m][:, c, cols],
                 op0=ALU.mult,
                 op1=ALU.add,
             )
 
-        def store(h, m, c, c0, w):
-            nc.sync.dma_start(
+        def store(h, m, c, c0, w, eng=nc.sync):
+            eng.dma_start(
                 out=out[c, m * P : (m + 1) * P, h * HALF_T + c0 : h * HALF_T + c0 + w],
                 in_=outs[h, m, c][:, c0 : c0 + w],
             )
 
         banks = {}
-        for g in range(G):
-            interleave(scopy, RE, g, 1)
-            if g == 0:
-                interleave(vcopy, RE, g, 0, 0, P)
-                interleave(vcopy, RE, g, 0, P, H2)
-                quantize(RE, g, 1, 0, 0, P)
-                quantize(RE, g, 1, 0, P, H2)
-            else:
-                interleave(vcopy, RE, g, 0)
-                quantize(RE, g, 1, 0)
-            quantize(RE, g, 1, 1)
-            for c in (RE, IM):
-                for m in range(MT):
-                    if g == 0:
-                        banks[m, c] = new_bank(2 * m + c)
-                    mm(banks[m, c], m, 0, RE, 1, RE if c == RE else IM, g, g == 0, False)
-            interleave(scopy, IM, g, 1)
-            interleave(vcopy, IM, g, 0)
-            for hf in (0, 1):
-                negate(IM, g, hf)
-                quantize(IM, g, 1, hf)
-                quantize(IM, g, -1, hf)
-            for m in range(MT):
-                mm(banks[m, RE], m, 0, IM, 1, IM, g, False, g == G - 1)
-                mm(banks[m, IM], m, 0, IM, -1, RE, g, False, g == G - 1)
+        def prepare_negated(g, hf):
+            negate(IM, g, hf)
+            quantize(IM, g, 1, hf)
+            quantize(IM, g, -1, hf)
+
+        interleave(vcopy, RE, 0, 0, 0, P)
+        interleave(vcopy, RE, 0, 0, P, H2)
+        quantize(RE, 0, 1, 0, 0, P)
+        quantize(RE, 0, 1, 0, P, H2)
+        for m in (0, 1):
+            banks[m, RE] = new_bank(2 * m + RE)
+            mm(banks[m, RE], m, 0, RE, 1, RE, 0, True, False)
+        interleave(vcopy, RE, 0, 1)
+        quantize(RE, 0, 1, 1)
+        for m in (2, 3):
+            banks[m, RE] = new_bank(2 * m + RE)
+            mm(banks[m, RE], m, 0, RE, 1, RE, 0, True, False)
+        step_t = psum.tile([P, P], BF16, name="bank7")
+        nc.tensor.transpose(step_t[:], step_rows[:], ident[:])
+        interleave(scopy, IM, 0, 1)
+        nc.scalar.copy(step_col[:], step_t[:, 0:MT])
+        for m in range(MT):
+            banks[m, IM] = new_bank(2 * m + IM)
+            mm(banks[m, IM], m, 0, RE, 1, IM, 0, True, False)
+        interleave(vcopy, IM, 0, 0)
+        for hf in (0, 1):
+            prepare_negated(0, hf)
+            for m in (2 * hf, 2 * hf + 1):
+                mm(banks[m, RE], m, 0, IM, 1, IM, 0, False, False)
+                mm(banks[m, IM], m, 0, IM, -1, RE, 0, False, False)
+        interleave(scopy, RE, 1, 1)
+        interleave(vcopy, RE, 1, 0)
+        for hf in (0, 1):
+            quantize(RE, 1, 1, hf)
+            for m in (2 * hf, 2 * hf + 1):
+                mm(banks[m, RE], m, 0, RE, 1, RE, 1, False, False)
+        interleave(scopy, IM, 1, 1)
+        interleave(vcopy, IM, 1, 0)
+        for hf in (0, 1):
+            prepare_negated(1, hf)
+            for m in (2 * hf, 2 * hf + 1):
+                mm(banks[m, IM], m, 0, IM, -1, RE, 1, False, False)
+        for m in range(MT):
+            mm(banks[m, RE], m, 0, IM, 1, IM, 1, False, True)
+            mm(banks[m, IM], m, 0, RE, 1, IM, 1, False, True)
         for m in range(MT):
             for c in (RE, IM):
                 finish(banks[m, c], 0, m, c, 0)
@@ -249,6 +270,11 @@ def tile_steering_residual_step_e2_kernel(
                 for nb in (0, 1):
                     bank = new_bank((4 * m + 2 * c + nb) % 8)
                     product(bank, m, c, HALF_T + nb * NT)
+                    if (m, c, nb) == (MT - 1, IM, 1):
+                        for i, eng in enumerate((nc.sync, nc.scalar)):
+                            finish(bank, 1, m, c, HALF_T + NT, i * NT // 2, NT // 2)
+                            store(1, m, c, NT + i * NT // 2, NT // 2, eng)
+                        continue
                     finish(bank, 1, m, c, HALF_T + nb * NT)
                     if m == MT - 1:
                         store(1, m, c, nb * NT, NT)

@@ -14,6 +14,7 @@ U8 = mybir.dt.uint8
 E4X4 = mybir.dt.float8_e4m3fn_x4
 E5X4 = mybir.dt.float8_e5m2_x4
 ALU = mybir.AluOpType
+ACT = mybir.ActivationFunctionType
 
 P = 128
 PACK = 4
@@ -68,11 +69,14 @@ def tile_steering_residual_step_e2_kernel(
                 rscale[part, i] = sb(f"rscale{part}{i}", [P, G, w], U8)
         amps = {}
         outs = {}
-        for h in (0, 1):
-            for m in range(MT):
-                amps[h, m] = sb(f"amp{h}{m}", [P, C, HALF_T], BF16)
-                for c in (RE, IM):
-                    outs[h, m, c] = sb(f"out{h}{m}{c}", [P, HALF_T], F32)
+        for m in range(MT):
+            amps[m] = sb(f"amp{m}", [P, C, T], BF16)
+            for c in (RE, IM):
+                if m < 2:
+                    for h in (0, 1):
+                        outs[m, c, h] = sb(f"out{m}{c}{h}", [P, HALF_T], F32)
+                else:
+                    outs[m, c] = sb(f"out{m}{c}", [P, T], F32)
         step_rows = sb("step_rows", [P, P], BF16)
         ident = sb("ident", [P, P], BF16)
         step_col = sb("step_col", [P, MT], F32)
@@ -90,27 +94,24 @@ def tile_steering_residual_step_e2_kernel(
                 out=words[part, g, i][:], in_=flat[:, PACK * c0 : PACK * (c0 + w)].bitcast(I32)
             )
 
-        def load_scales(eng, part, i):
+        def load_scales(eng, part, i, rows=(0, 1, 2, 3)):
             c0, w = schunks[i]
-            for q in range(4):
+            for q in rows:
                 eng.dma_start(
                     out=rscale[part, i][32 * q : 32 * q + 4, :, :].bitcast(I32),
                     in_=scales_in[part][:, 4 * q : 4 * q + 4, c0 : c0 + w].rearrange("g q n -> q g n").bitcast(I32),
                 )
 
-        def load_amp(h, m):
-            nc.sync.dma_start(
-                out=amps[h, m][:],
-                in_=amp[:, m * P : (m + 1) * P, h * HALF_T : (h + 1) * HALF_T].rearrange("c p n -> p c n"),
-            )
+        def load_amp(m):
+            nc.sync.dma_start(out=amps[m][:], in_=amp[:, m * P : (m + 1) * P, :].rearrange("c p n -> p c n"))
 
         def clear_scales(part, i):
             nc.vector.memset(rscale[part, i][:].rearrange("p g n -> p (g n)").bitcast(I32), 0)
 
         load_a(RE, 0)
-        nc.vector.memset(step_rows[:], 0.0)
         clear_scales(RE, 0)
         clear_scales(IM, 0)
+        nc.vector.memset(step_rows[:], 0.0)
         clear_scales(RE, 1)
         clear_scales(IM, 1)
         nc.gpsimd.dma_start(out=step_rows[0:MT, :], in_=step.rearrange("(m p) -> m p", p=P))
@@ -130,13 +131,14 @@ def tile_steering_residual_step_e2_kernel(
         load_words(RE, 1, 1)
         load_scales(nc.sync, IM, 1)
         load_words(IM, 1, 1)
-        for m in range(MT):
-            load_amp(0, m)
-        for g in range(G):
-            for part in (RE, IM):
-                load_words(part, g, 2)
-        for m in range(MT):
-            load_amp(1, m)
+        load_words(RE, 0, 2)
+        load_words(IM, 0, 2)
+        load_words(RE, 1, 2)
+        load_words(IM, 1, 2)
+        load_amp(0)
+        load_amp(1)
+        load_amp(2)
+        load_amp(3)
 
         H2 = D // 2
 
@@ -185,22 +187,33 @@ def tile_steering_residual_step_e2_kernel(
         def new_bank(k):
             return psum.tile([P, NT], F32, name=f"bank{k}")
 
-        def finish(bank, h, m, c, n0, lo=0, w=NT):
-            cols = slice(n0 - h * HALF_T + lo, n0 - h * HALF_T + lo + w)
+        def out_cols(m, c, n0, w):
+            if m < 2:
+                h = n0 // HALF_T
+                return outs[m, c, h][:, n0 - h * HALF_T : n0 - h * HALF_T + w]
+            return outs[m, c][:, n0 : n0 + w]
+
+        def scale_out(bank, m, c, n0):
+            nc.scalar.activation(
+                out=out_cols(m, c, n0, NT), in_=bank[:], func=ACT.Copy, scale=step_col[:, m : m + 1]
+            )
+
+        def add_amp(m, c):
+            half = out_cols(m, c, 0, HALF_T)
+            nc.vector.tensor_tensor(out=half, in0=half, in1=amps[m][:, c, 0:HALF_T], op=ALU.add)
+
+        def finish(bank, m, c, n0, lo=0, w=NT):
             nc.vector.scalar_tensor_tensor(
-                out=outs[h, m, c][:, cols],
+                out=out_cols(m, c, n0 + lo, w),
                 in0=bank[:, lo : lo + w],
                 scalar=step_col[:, m : m + 1],
-                in1=amps[h, m][:, c, cols],
+                in1=amps[m][:, c, n0 + lo : n0 + lo + w],
                 op0=ALU.mult,
                 op1=ALU.add,
             )
 
-        def store(h, m, c, c0, w, eng=nc.sync):
-            eng.dma_start(
-                out=out[c, m * P : (m + 1) * P, h * HALF_T + c0 : h * HALF_T + c0 + w],
-                in_=outs[h, m, c][:, c0 : c0 + w],
-            )
+        def store(m, c, n0, w, eng=nc.sync):
+            eng.dma_start(out=out[c, m * P : (m + 1) * P, n0 : n0 + w], in_=out_cols(m, c, n0, w))
 
         banks = {}
         def prepare_negated(g, hf):
@@ -241,16 +254,15 @@ def tile_steering_residual_step_e2_kernel(
                 mm(banks[m, RE], m, 0, RE, 1, RE, 1, False, False)
         interleave(scopy, IM, 1, 1)
         interleave(vcopy, IM, 1, 0)
+        for m in range(MT):
+            mm(banks[m, IM], m, 0, RE, 1, IM, 1, False, False)
         for hf in (0, 1):
             prepare_negated(1, hf)
             for m in (2 * hf, 2 * hf + 1):
-                mm(banks[m, IM], m, 0, IM, -1, RE, 1, False, False)
-        for m in range(MT):
-            mm(banks[m, RE], m, 0, IM, 1, IM, 1, False, True)
-            mm(banks[m, IM], m, 0, RE, 1, IM, 1, False, True)
-        for m in range(MT):
-            for c in (RE, IM):
-                finish(banks[m, c], 0, m, c, 0)
+                mm(banks[m, RE], m, 0, IM, 1, IM, 1, False, True)
+                scale_out(banks[m, RE], m, RE, 0)
+                mm(banks[m, IM], m, 0, IM, -1, RE, 1, False, True)
+                scale_out(banks[m, IM], m, IM, 0)
 
         def product(bank, m, c, n0):
             order = [(apart, g) for apart in (RE, IM) for g in range(G)]
@@ -263,20 +275,30 @@ def tile_steering_residual_step_e2_kernel(
             for c in (RE, IM):
                 bank = new_bank(2 * m + c)
                 product(bank, m, c, NT)
-                finish(bank, 0, m, c, NT)
-                store(0, m, c, 0, HALF_T)
-        for m in range(MT):
+                scale_out(bank, m, c, NT)
+        for m in (0, 1):
             for c in (RE, IM):
+                add_amp(m, c)
+                store(m, c, 0, HALF_T)
+        add_amp(2, RE)
+        add_amp(2, IM)
+        for k, m in enumerate((2, 3, 0, 1)):
+            for c in (RE, IM):
+                last = (m, c) == (1, IM)
                 for nb in (0, 1):
-                    bank = new_bank((4 * m + 2 * c + nb) % 8)
-                    product(bank, m, c, HALF_T + nb * NT)
-                    if (m, c, nb) == (MT - 1, IM, 1):
-                        for i, eng in enumerate((nc.sync, nc.scalar)):
-                            finish(bank, 1, m, c, HALF_T + NT, i * NT // 2, NT // 2)
-                            store(1, m, c, NT + i * NT // 2, NT // 2, eng)
-                        continue
-                    finish(bank, 1, m, c, HALF_T + nb * NT)
-                    if m == MT - 1:
-                        store(1, m, c, nb * NT, NT)
-                if m < MT - 1:
-                    store(1, m, c, 0, HALF_T)
+                    n0 = HALF_T + nb * NT
+                    bank = new_bank((4 * k + 2 * c + nb) % 8)
+                    product(bank, m, c, n0)
+                    if not (last and nb == 1):
+                        finish(bank, m, c, n0)
+                if m >= 2:
+                    if m == 2:
+                        add_amp(3, c)
+                    store(m, c, 0, T)
+                elif not last:
+                    store(m, c, HALF_T, HALF_T)
+                else:
+                    store(m, c, HALF_T, NT)
+                    for i, eng in enumerate((nc.sync, nc.scalar)):
+                        finish(bank, m, c, n0, i * NT // 2, NT // 2)
+                        store(m, c, n0 + i * NT // 2, NT // 2, eng)

from contextlib import ExitStack

import concourse.mybir as mybir
from concourse.masks import make_identity

M, D, T, C = 1024, 512, 2048, 2
FLOPS = 4 * 2 * M * D * T

F32 = mybir.dt.float32
BF16 = mybir.dt.bfloat16
I32 = mybir.dt.int32
U32 = mybir.dt.uint32
U8 = mybir.dt.uint8
E4X4 = mybir.dt.float8_e4m3fn_x4
E5X4 = mybir.dt.float8_e5m2_x4
ALU = mybir.AluOpType
ACT = mybir.ActivationFunctionType

P = 128
PACK = 4
K_PASS = P * PACK
G = M // K_PASS
MT = D // P
NT = 512
HALF_T = T // 2
RE, IM = 0, 1


def tile_steering_residual_step_e2_kernel(
    tc, a_re, a_im, r_re_words, r_re_scales, r_im_words, r_im_scales, step, amp, out
):
    nc = tc.nc
    a_in = (a_re, a_im)
    words_in = (r_re_words, r_im_words)
    scales_in = (r_re_scales, r_im_scales)

    with ExitStack() as ctx:
        keep = ctx.enter_context(tc.tile_pool(name="keep", bufs=1))
        psum = ctx.enter_context(tc.psum_pool(name="psum", bufs=1))
        ctx.enter_context(tc.manual_schedule())

        def sb(label, shape, dtype):
            return keep.tile(shape, dtype, name=label, align_bytes=64)

        raw = {}
        grp = {}
        codes = {}
        cscale = {}
        for part in (RE, IM):
            for g in range(G):
                raw[part, g] = sb(f"raw{part}{g}", [P, PACK, D], BF16)
                for sign in ((1,) if part == RE else (1, -1)):
                    for hf in (0, 1):
                        key = (part, g, sign, hf)
                        lab = f"{part}{g}{sign + 1}{hf}"
                        grp[key] = sb("grp" + lab, [P, D // 2, PACK], BF16)
                        codes[key] = sb("codes" + lab, [P, D // 2], U32)
                        cscale[key] = sb("cscale" + lab, [P, D // 2], U8)
        chunks = ((0, 512), (512, 512), (1024, 1024))
        words = {}
        for part in (RE, IM):
            for g in range(G):
                for i, (c0, w) in enumerate(chunks):
                    words[part, g, i] = sb(f"words{part}{g}{i}", [P, w], I32)
        schunks = ((0, 512), (512, 1536))
        rscale = {}
        for part in (RE, IM):
            for i, (c0, w) in enumerate(schunks):
                rscale[part, i] = sb(f"rscale{part}{i}", [P, G, w], U8)
        amps = {}
        outs = {}
        for m in range(MT):
            amps[m] = sb(f"amp{m}", [P, C, T], BF16)
            for c in (RE, IM):
                if m < 2:
                    for h in (0, 1):
                        outs[m, c, h] = sb(f"out{m}{c}{h}", [P, HALF_T], F32)
                else:
                    outs[m, c] = sb(f"out{m}{c}", [P, T], F32)
        step_rows = sb("step_rows", [P, P], BF16)
        ident = sb("ident", [P, P], BF16)
        step_col = sb("step_col", [P, MT], F32)

        def load_a(part, g):
            nc.sync.dma_start(
                out=raw[part, g][:],
                in_=a_in[part][g * K_PASS : (g + 1) * K_PASS, :].rearrange("(p j) d -> p j d", j=PACK),
            )

        def load_words(part, g, i):
            c0, w = chunks[i]
            flat = words_in[part][g].rearrange("p n t -> p (n t)")
            nc.sync.dma_start(
                out=words[part, g, i][:], in_=flat[:, PACK * c0 : PACK * (c0 + w)].bitcast(I32)
            )

        def load_scales(eng, part, i, rows=(0, 1, 2, 3)):
            c0, w = schunks[i]
            for q in rows:
                eng.dma_start(
                    out=rscale[part, i][32 * q : 32 * q + 4, :, :].bitcast(I32),
                    in_=scales_in[part][:, 4 * q : 4 * q + 4, c0 : c0 + w].rearrange("g q n -> q g n").bitcast(I32),
                )

        def load_amp(m):
            nc.sync.dma_start(out=amps[m][:], in_=amp[:, m * P : (m + 1) * P, :].rearrange("c p n -> p c n"))

        def clear_scales(part, i):
            nc.vector.memset(rscale[part, i][:].rearrange("p g n -> p (g n)").bitcast(I32), 0)

        load_a(RE, 0)
        clear_scales(RE, 0)
        clear_scales(IM, 0)
        nc.vector.memset(step_rows[:], 0.0)
        clear_scales(RE, 1)
        clear_scales(IM, 1)
        nc.gpsimd.dma_start(out=step_rows[0:MT, :], in_=step.rearrange("(m p) -> m p", p=P))
        make_identity(nc, ident[:])
        load_scales(nc.sync, RE, 0)
        load_words(RE, 0, 0)
        load_words(IM, 0, 0)
        load_a(IM, 0)
        load_scales(nc.sync, IM, 0)
        load_a(RE, 1)
        load_a(IM, 1)
        load_words(RE, 1, 0)
        load_words(IM, 1, 0)
        load_words(RE, 0, 1)
        load_scales(nc.sync, RE, 1)
        load_words(IM, 0, 1)
        load_words(RE, 1, 1)
        load_scales(nc.sync, IM, 1)
        load_words(IM, 1, 1)
        load_words(RE, 0, 2)
        load_words(IM, 0, 2)
        load_words(RE, 1, 2)
        load_words(IM, 1, 2)
        load_amp(0)
        load_amp(1)
        load_amp(2)
        load_amp(3)

        H2 = D // 2

        def interleave(eng_copy, part, g, hf, lo=0, hi=H2):
            eng_copy(
                out=grp[part, g, 1, hf][:, lo:hi, :],
                in_=raw[part, g][:, :, hf * H2 + lo : hf * H2 + hi].rearrange("p j d -> p d j"),
            )

        def scopy(out, in_):
            nc.scalar.copy(out, in_)

        def vcopy(out, in_):
            nc.vector.tensor_copy(out=out, in_=in_)

        def negate(part, g, hf):
            nc.vector.tensor_scalar(
                out=grp[part, g, -1, hf][:], in0=grp[part, g, 1, hf][:], scalar1=-1.0, scalar2=None, op0=ALU.mult
            )

        def quantize(part, g, sign, hf, lo=0, hi=H2):
            key = (part, g, sign, hf)
            nc.vector.quantize_mx(
                out=codes[key][:, lo:hi].bitcast(E4X4),
                scales=cscale[key][:, lo:hi],
                in_=grp[key][:, lo:hi, :].rearrange("p d j -> p (d j)"),
            )

        def mm(bank, m, n0, apart, sign, rpart, g, start, stop):
            key = (apart, g, sign, m // 2)
            ac = slice((m % 2) * P, (m % 2 + 1) * P)
            i = 0 if n0 < 512 else (1 if n0 < 1024 else 2)
            wc = n0 - chunks[i][0]
            si = 0 if n0 < 512 else 1
            sc = n0 - schunks[si][0]
            nc.tensor.matmul_mx(
                out=bank[:],
                lhsT=codes[key][:, ac].bitcast(E4X4),
                lhsT_scale=cscale[key][:, ac],
                rhs=words[rpart, g, i][:, wc : wc + NT].bitcast(E5X4),
                rhs_scale=rscale[rpart, si][:, g, sc : sc + NT],
                start=start,
                stop=stop,
            )

        def new_bank(k):
            return psum.tile([P, NT], F32, name=f"bank{k}")

        def out_cols(m, c, n0, w):
            if m < 2:
                h = n0 // HALF_T
                return outs[m, c, h][:, n0 - h * HALF_T : n0 - h * HALF_T + w]
            return outs[m, c][:, n0 : n0 + w]

        def scale_out(bank, m, c, n0):
            nc.scalar.activation(
                out=out_cols(m, c, n0, NT), in_=bank[:], func=ACT.Copy, scale=step_col[:, m : m + 1]
            )

        def add_amp(m, c):
            half = out_cols(m, c, 0, HALF_T)
            nc.vector.tensor_tensor(out=half, in0=half, in1=amps[m][:, c, 0:HALF_T], op=ALU.add)

        def finish(bank, m, c, n0, lo=0, w=NT):
            nc.vector.scalar_tensor_tensor(
                out=out_cols(m, c, n0 + lo, w),
                in0=bank[:, lo : lo + w],
                scalar=step_col[:, m : m + 1],
                in1=amps[m][:, c, n0 + lo : n0 + lo + w],
                op0=ALU.mult,
                op1=ALU.add,
            )

        def store(m, c, n0, w, eng=nc.sync):
            eng.dma_start(out=out[c, m * P : (m + 1) * P, n0 : n0 + w], in_=out_cols(m, c, n0, w))

        banks = {}
        def prepare_negated(g, hf):
            negate(IM, g, hf)
            quantize(IM, g, 1, hf)
            quantize(IM, g, -1, hf)

        interleave(vcopy, RE, 0, 0, 0, P)
        interleave(vcopy, RE, 0, 0, P, H2)
        quantize(RE, 0, 1, 0, 0, P)
        quantize(RE, 0, 1, 0, P, H2)
        for m in (0, 1):
            banks[m, RE] = new_bank(2 * m + RE)
            mm(banks[m, RE], m, 0, RE, 1, RE, 0, True, False)
        interleave(vcopy, RE, 0, 1)
        quantize(RE, 0, 1, 1)
        for m in (2, 3):
            banks[m, RE] = new_bank(2 * m + RE)
            mm(banks[m, RE], m, 0, RE, 1, RE, 0, True, False)
        step_t = psum.tile([P, P], BF16, name="bank7")
        nc.tensor.transpose(step_t[:], step_rows[:], ident[:])
        interleave(scopy, IM, 0, 1)
        nc.scalar.copy(step_col[:], step_t[:, 0:MT])
        for m in range(MT):
            banks[m, IM] = new_bank(2 * m + IM)
            mm(banks[m, IM], m, 0, RE, 1, IM, 0, True, False)
        interleave(vcopy, IM, 0, 0)
        for hf in (0, 1):
            prepare_negated(0, hf)
            for m in (2 * hf, 2 * hf + 1):
                mm(banks[m, RE], m, 0, IM, 1, IM, 0, False, False)
                mm(banks[m, IM], m, 0, IM, -1, RE, 0, False, False)
        interleave(scopy, RE, 1, 1)
        interleave(vcopy, RE, 1, 0)
        for hf in (0, 1):
            quantize(RE, 1, 1, hf)
            for m in (2 * hf, 2 * hf + 1):
                mm(banks[m, RE], m, 0, RE, 1, RE, 1, False, False)
        interleave(scopy, IM, 1, 1)
        interleave(vcopy, IM, 1, 0)
        for m in range(MT):
            mm(banks[m, IM], m, 0, RE, 1, IM, 1, False, False)
        for hf in (0, 1):
            prepare_negated(1, hf)
            for m in (2 * hf, 2 * hf + 1):
                mm(banks[m, RE], m, 0, IM, 1, IM, 1, False, True)
                scale_out(banks[m, RE], m, RE, 0)
                mm(banks[m, IM], m, 0, IM, -1, RE, 1, False, True)
                scale_out(banks[m, IM], m, IM, 0)

        def product(bank, m, c, n0):
            order = [(apart, g) for apart in (RE, IM) for g in range(G)]
            for i, (apart, g) in enumerate(order):
                sign = -1 if (apart == IM and c == IM) else 1
                rpart = apart if c == RE else 1 - apart
                mm(bank, m, n0, apart, sign, rpart, g, i == 0, i == len(order) - 1)

        for m in range(MT):
            for c in (RE, IM):
                bank = new_bank(2 * m + c)
                product(bank, m, c, NT)
                scale_out(bank, m, c, NT)
        for m in (0, 1):
            for c in (RE, IM):
                add_amp(m, c)
                store(m, c, 0, HALF_T)
        add_amp(2, RE)
        add_amp(2, IM)
        for k, m in enumerate((2, 3, 0, 1)):
            for c in (RE, IM):
                last = (m, c) == (1, IM)
                for nb in (0, 1):
                    n0 = HALF_T + nb * NT
                    bank = new_bank((4 * k + 2 * c + nb) % 8)
                    product(bank, m, c, n0)
                    if not (last and nb == 1):
                        finish(bank, m, c, n0)
                if m >= 2:
                    if m == 2:
                        add_amp(3, c)
                    store(m, c, 0, T)
                elif not last:
                    store(m, c, HALF_T, HALF_T)
                else:
                    store(m, c, HALF_T, NT)
                    for i, eng in enumerate((nc.sync, nc.scalar)):
                        finish(bank, m, c, n0, i * NT // 2, NT // 2)
                        store(m, c, n0 + i * NT // 2, NT // 2, eng)
